import numpy as np
import ml_dtypes


def mxq(x, axis, fmt="e4m3"):
    dtype, down = {"e4m3": (ml_dtypes.float8_e4m3fn, 7), "e5m2": (ml_dtypes.float8_e5m2, 14)}[fmt]
    v = np.moveaxis(np.asarray(x, np.float32).astype(ml_dtypes.bfloat16).astype(np.float64), axis, -1)
    blocks = v.reshape(v.shape[:-1] + (-1, 32))
    amax = np.abs(blocks).max(-1, keepdims=True)
    byte = np.maximum(np.where(amax > 0, np.frexp(amax)[1] - 1 + 127, 0) - down, 1)
    scale = np.exp2(byte - 127.0)
    codes = (blocks / scale).astype(np.float32).astype(dtype).astype(np.float64)
    return np.moveaxis((codes * scale).reshape(v.shape), -1, axis)


WIDE = False


def mx_kscale(k):
    if not WIDE:
        return np.ones(k)
    levels = np.array([10, -10, 5, -5, 0])
    if k % 512:
        return np.exp2(np.random.permutation(np.resize(levels, k // 32))).repeat(32)
    a = np.empty((k // 512, 16))
    for p in range(k // 512):
        a[p, :8] = np.random.permutation(np.resize(levels, 8))
        for g in range(8):
            far = levels[np.abs(levels - a[p, g]) >= 10]
            a[p, g + 8] = far[np.random.randint(len(far))]
    return np.exp2(a.ravel()).repeat(32)


def f64(x):
    return np.asarray(x).astype(np.float64)


def striped(idx):
    return np.tile(idx.reshape(-1, 16).T, (8, 1)).astype(np.uint16)


def unstriped(offs):
    return offs[:16].T.reshape(-1).astype(np.int64)


E2M1 = np.array([0.0, 0.5, 1.0, 1.5, 2.0, 3.0, 4.0, 6.0, -0.0, -0.5, -1.0, -1.5, -2.0, -3.0, -4.0, -6.0])


def pack_weight(w, fmt):
    k, n = w.shape
    w = f64(np.asarray(w, np.float32).astype(ml_dtypes.bfloat16)).reshape(k // 32, 32, n)
    amax = np.abs(w).max(1)
    if fmt == "e4m3":
        byte = np.frexp(amax)[1] - 1 + 127 - 7
    else:
        mant, ex = np.frexp(amax / 6.0)
        byte = np.where(mant > 0.5, ex, ex - 1) + 127
    byte = np.clip(np.where(amax > 0, byte, 1), 1, 254)
    scaled = (w * np.exp2(127.0 - byte)[:, None, :]).reshape(k, n).astype(np.float32)
    by_word = np.ascontiguousarray(scaled.reshape(k // 512, 128, 4, n).transpose(0, 1, 3, 2))
    if fmt == "e4m3":
        words = by_word.astype(ml_dtypes.float8_e4m3fn).view(np.uint8)
    else:
        c = by_word.astype(ml_dtypes.float4_e2m1fn).view(np.uint8) & 0xF
        words = (c[..., 0::2] | (c[..., 1::2] << 4)).reshape(k // 512, 128, 2 * n)
    return np.ascontiguousarray(words), np.ascontiguousarray(byte.astype(np.uint8).reshape(k // 512, 16, n))


def unpack_weight(words, scales, fmt):
    g, _, n = scales.shape
    words = np.ascontiguousarray(words).reshape(g, 128, n, -1)
    if fmt == "e4m3":
        vals = words.view(ml_dtypes.float8_e4m3fn).astype(np.float64)
    else:
        nib = np.empty((g, 128, n, 4), np.uint8)
        nib[..., 0::2] = words & 0xF
        nib[..., 1::2] = words >> 4
        vals = E2M1[nib]
    vals = vals * np.repeat(np.exp2(scales.astype(np.float64) - 127.0), 8, axis=1)[..., None]
    return vals.transpose(0, 1, 3, 2).reshape(g * 512, n)


def gelu(v):
    return 0.5 * v * (1.0 + np.tanh(np.sqrt(2.0 / np.pi) * (v + 0.044715 * v**3)))


K, H, N, T, S, P = 1536, 1024, 512, 2048, 1024, 512

def setup_inputs():
    n = np.random.standard_normal
    s = mx_kscale(K)[:, None]
    u = mx_kscale(H)[:, None]
    tab_words, tab_scales = pack_weight(n((K, T)) * s, "e4m3")
    w4_words, w4_scales = pack_weight(n((H, N)) / np.sqrt(H) / u, "e2m1")
    perm = np.random.permutation(S)
    return {
        "tab_words": tab_words, "tab_scales": tab_scales,
        "offs": striped(np.random.permutation(T)[:S]),
        "pos1": striped(perm[:P]),
        "pos2": striped(perm[P:]),
        "w1": (0.85 * n((K, H)) / np.sqrt(K) / s).astype(np.float32),
        "tint": (6.0 * n((H, P))).astype(np.float32),
        "skip": np.random.uniform(0.5, 1.5, H).astype(np.float32),
        "wgs": np.exp(0.3 * n((128, P))).astype(np.float32),
        "gain": (np.random.uniform(0.6, 1.8, H) * u[:, 0]).astype(np.float32),
        "w4_words": w4_words, "w4_scales": w4_scales,
    }

def reference(tab_words, tab_scales, offs, pos1, pos2, w1, tint, skip, wgs, gain, w4_words, w4_scales):
    v = unpack_weight(tab_words, tab_scales, "e4m3")[:, unstriped(offs)]
    w4 = unpack_weight(w4_words, w4_scales, "e2m1")
    h = mxq(f64(w1), 0, "e4m3").T @ v
    top = h.max(axis=1)
    a = np.exp(h[:, unstriped(pos1)] - top[:, None]) * f64(tint)
    page = f64(skip)[:, None] * h
    page[:, unstriped(pos2)] = np.tile(f64(wgs), (H // 128, 1)) * a
    b = mxq(f64(gain)[:, None] * page, 0, "e4m3")
    return w4.T @ b

@@ -1,0 +1,320 @@
+from contextlib import ExitStack
+
+import concourse.mybir as mybir
+
+K, H, N, T, S, M = 1536, 1024, 512, 2048, 1024, 512
+FLOPS = 2 * K * H * S + 2 * H * N * S
+
+F32 = mybir.dt.float32
+BF16 = mybir.dt.bfloat16
+I32 = mybir.dt.int32
+U32 = mybir.dt.uint32
+U16 = mybir.dt.uint16
+U8 = mybir.dt.uint8
+FP8X4 = mybir.dt.float8_e4m3fn_x4
+FP4X4 = mybir.dt.float4_e2m1fn_x4
+ALU = mybir.AluOpType
+ACT = mybir.ActivationFunctionType
+
+P = 128
+PACK = 4
+PASS = P * PACK
+K_PASSES = K // PASS
+R_PASSES = H // PASS
+BANK = 512
+HALVES = S // BANK
+ROW_TILES = R_PASSES * PACK
+QUADRANTS = 4
+PIECES = ((0, 256), (256, 768), (768, 1024))
+SCALAR_SHARE = 64
+
+
+def tile_list_tarnish_bloom_rewrite_kernel(
+    tc, tab_words, tab_scales, offs, pos1, pos2, w1, tint, skip, wgs, gain, w4_words, w4_scales, out
+):
+    nc = tc.nc
+    with ExitStack() as ctx:
+        held = ctx.enter_context(tc.tile_pool(name="held", bufs=1))
+        ring = ctx.enter_context(tc.tile_pool(name="ring", bufs=3))
+        psum = ctx.enter_context(tc.psum_pool(name="psum", bufs=1))
+
+        offs_sb = held.tile([P, S // 16], U16, name="offs_sb")
+        pos1_sb = held.tile([P, M // 16], U16, name="pos1_sb")
+        pos2_sb = held.tile([P, M // 16], U16, name="pos2_sb")
+        tab_sb = [held.tile([P, T], I32, name="tab%d" % a, align_bytes=64) for a in range(K_PASSES)]
+        tab_sc = held.tile([P, T], U8, name="tab_sc", align_bytes=64)
+        v_words = [held.tile([P, S], U32, name="v_words%d" % a, align_bytes=64) for a in range(K_PASSES)]
+        v_sc = held.tile([P, S], U8, name="v_sc", align_bytes=64)
+        w1_codes = {}
+        w1_sc = {}
+        w1_raw = {}
+        for b in range(R_PASSES):
+            for a in range(K_PASSES):
+                w1_codes[b, a] = held.tile([P, PASS], U32, name="w1_codes%d_%d" % (b, a), align_bytes=64)
+                w1_sc[b, a] = held.tile([P, PASS], U8, name="w1_sc%d_%d" % (b, a), align_bytes=64)
+        tint_sb = {}
+        wgs_sb = {}
+        skip_sb = held.tile([P, R_PASSES, PACK], F32, name="skip_sb")
+        gain_sb = held.tile([P, R_PASSES, PACK], F32, name="gain_sb")
+        w4_sb = held.tile([P, R_PASSES, 2 * N], U8, name="w4_sb", align_bytes=64)
+        w4_sc = held.tile([P, R_PASSES, N], U8, name="w4_sc", align_bytes=64)
+        b_codes = [held.tile([P, S], U32, name="b_codes%d" % b, align_bytes=64) for b in range(R_PASSES)]
+        b_sc = [held.tile([P, S], U8, name="b_sc%d" % b, align_bytes=64) for b in range(R_PASSES)]
+        b_woven = [None] * R_PASSES
+        b_rows = [held.tile([P, PACK, S], BF16, name="b_rows%d" % b, align_bytes=64) for b in range(R_PASSES)]
+
+        nc.gpsimd.memset(tab_sc[:].bitcast(U32), 0)
+
+        def load_tab(a):
+            nc.sync.dma_start(out=tab_sb[a][:], in_=tab_words[a].rearrange("p t i -> p (t i)").bitcast(I32))
+
+        def load_w1(b, a, pieces):
+            width = PASS // pieces
+            w1_raw[b, a] = []
+            for u in range(pieces):
+                raw = ring.tile([P, PACK, width], F32, name="w1_raw", bufs=5)
+                c0 = b * PASS + u * width
+                rows = w1[a * PASS : (a + 1) * PASS, c0 : c0 + width]
+                nc.sync.dma_start(out=raw[:], in_=rows.rearrange("(p i) c -> p i c", i=PACK))
+                w1_raw[b, a].append(raw)
+
+        def load_tint(b, t0, t1):
+            rows = tint[b * PASS : (b + 1) * PASS, :].rearrange("(p t) m -> p t m", t=PACK)
+            tile = held.tile([P, t1 - t0, M], F32, name="tint%d_%d" % (b, t0))
+            nc.sync.dma_start(out=tile[:], in_=rows[:, t0:t1, :])
+            for t in range(t0, t1):
+                tint_sb[PACK * b + t] = tile[:, t - t0, :]
+
+        def load_wgs(t0, t1):
+            rows = wgs.rearrange("(q t) m -> q t m", t=PACK)
+            tile = held.tile([P, t1 - t0, M], F32, name="wgs%d" % t0)
+            for quad in (0, 2, 1, 3):
+                nc.sync.dma_start(out=tile[32 * quad : 32 * quad + 32, :, :], in_=rows[:, t0:t1, :])
+            for t in range(t0, t1):
+                wgs_sb[t] = tile[:, t - t0, :]
+
+        nc.sync.dma_start(offs_sb[:], offs)
+        load_tab(0)
+        nc.sync.dma_start(pos1_sb[:], pos1)
+        nc.sync.dma_start(pos2_sb[:], pos2)
+        for quad in range(QUADRANTS):
+            nc.sync.dma_start(
+                out=tab_sc[32 * quad : 32 * quad + 4 * K_PASSES, :].bitcast(I32),
+                in_=tab_scales[:, 4 * quad : 4 * quad + 4, :].bitcast(I32),
+            )
+        load_w1(0, 0, 1)
+        load_tab(1)
+        load_tab(2)
+        load_w1(0, 1, 1)
+        load_w1(0, 2, 2)
+        nc.sync.dma_start(out=skip_sb[:], in_=skip.rearrange("(b p t) -> p b t", p=P, t=PACK))
+        load_w1(1, 0, 1)
+        load_tint(0, 0, 1)
+        load_wgs(0, 1)
+        load_w1(1, 1, 1)
+        load_tint(0, 1, PACK)
+        load_wgs(1, PACK)
+        load_w1(1, 2, 1)
+        nc.sync.dma_start(out=gain_sb[:], in_=gain.rearrange("(b p t) -> p b t", p=P, t=PACK))
+        load_tint(1, 0, PACK)
+
+        def gather_words(a):
+            nc.vector.tensor_copy(out=v_words[a][:], in_=tab_sb[a][:].bitcast(U32).indirect(offs_sb[:]))
+
+        def round_w1(b, a):
+            grouped = ring.tile([P, PACK * PASS], BF16, name="w1_bf", align_bytes=64, bufs=3)
+            dst = grouped[:].rearrange("p (t m i) -> p m i t", t=PACK, i=PACK)
+            srcs = [raw[:].rearrange("p i (m t) -> p m i t", t=PACK) for raw in w1_raw[b, a]]
+            if len(srcs) == 2:
+                half = P // 2
+                nc.scalar.copy(out=dst[:, :half], in_=srcs[0])
+                nc.vector.tensor_copy(out=dst[:, half:], in_=srcs[1])
+            elif (b, a) == (0, 1):
+                nc.scalar.copy(out=dst[:, :SCALAR_SHARE], in_=srcs[0][:, :SCALAR_SHARE])
+                nc.vector.tensor_copy(out=dst[:, SCALAR_SHARE:], in_=srcs[0][:, SCALAR_SHARE:])
+            else:
+                nc.scalar.copy(out=dst[:, : P // 2], in_=srcs[0][:, : P // 2])
+                nc.scalar.copy(out=dst[:, P // 2 :], in_=srcs[0][:, P // 2 :])
+            return grouped
+
+        def quantise_w1(b, a, pieces):
+            grouped = round_w1(b, a)
+            width = PASS // pieces
+            for u in range(pieces):
+                cols = slice(u * width, (u + 1) * width)
+                nc.vector.quantize_mx(
+                    out=w1_codes[b, a][:, cols].bitcast(FP8X4),
+                    scales=w1_sc[b, a][:, cols],
+                    in_=grouped[:, PACK * u * width : PACK * (u + 1) * width],
+                )
+
+        gather_words(0)
+        nc.vector.tensor_copy(out=v_sc[:], in_=tab_sc[:].indirect(offs_sb[:]))
+        gather_words(1)
+        quantise_w1(0, 0, 1)
+        gather_words(2)
+        quantise_w1(0, 1, 1)
+        quantise_w1(0, 2, PACK)
+
+        quantise_w1(1, 0, 1)
+        nc.gpsimd.memset(w4_sc[:].rearrange("p b n -> p (b n)").bitcast(U32), 0)
+        for b in range(R_PASSES):
+            nc.sync.dma_start(out=w4_sb[:, b, :].bitcast(I32), in_=w4_words[b].bitcast(I32))
+        for quad in range(QUADRANTS):
+            nc.sync.dma_start(
+                out=w4_sc[32 * quad : 32 * quad + 4, :, :].bitcast(I32),
+                in_=w4_scales[:, 4 * quad : 4 * quad + 4, :].rearrange("b r n -> r b n").bitcast(I32),
+            )
+
+        h_sb = {}
+        looked = {}
+        page = {}
+        acc = {}
+
+        def first_product(i):
+            b, t = divmod(i, PACK)
+            cols = slice(t * P, (t + 1) * P)
+            h_sb[i] = ring.tile([P, S], F32, name="h_sb")
+            tops = ring.tile([P, HALVES], F32, name="tops")
+            neg_top = ring.tile([P, 1], F32, name="neg_top")
+            banks = [psum.tile([P, BANK], F32, name="bank%d" % (HALVES * (i % PACK) + c)) for c in range(HALVES)]
+            for a in range(K_PASSES):
+                for c in range(HALVES):
+                    js = slice(c * BANK, (c + 1) * BANK)
+                    nc.tensor.matmul_mx(
+                        out=banks[c][:],
+                        lhsT=w1_codes[b, a][:, cols].bitcast(FP8X4),
+                        lhsT_scale=w1_sc[b, a][:, cols],
+                        rhs=v_words[a][:, js].bitcast(FP8X4),
+                        rhs_scale=v_sc[4 * a : P, js],
+                        start=(a == 0),
+                        stop=(a == K_PASSES - 1),
+                    )
+            for c in range(HALVES):
+                nc.vector.tensor_scalar(
+                    out=h_sb[i][:, c * BANK : (c + 1) * BANK],
+                    in0=banks[c][:],
+                    scalar1=1.0,
+                    scalar2=tops[:, 0:1] if c else None,
+                    op0=ALU.mult,
+                    op1=ALU.max,
+                    accum_out=tops[:, c : c + 1],
+                )
+            nc.scalar.activation(out=neg_top[:], in_=tops[:, 1:2], func=ACT.Copy, scale=-1.0)
+            looked[i] = ring.tile([P, M], F32, name="looked", bufs=4)
+            nc.scalar.activation(out=looked[i][:], in_=h_sb[i][:].indirect(pos1_sb[:]), func=ACT.Exp, bias=neg_top[:])
+            page[i] = ring.tile([P, S], F32, name="page", bufs=5)
+            nc.scalar.activation(out=page[i][:], in_=h_sb[i][:], func=ACT.Copy, scale=skip_sb[:, b, t : t + 1])
+
+        factor = {}
+
+        def make_factor(i):
+            t = i % PACK
+            factor[i] = ring.tile([P, M], F32, name="factor", bufs=3)
+            nc.gpsimd.tensor_tensor(
+                out=factor[i][:], in0=tint_sb[i], in1=wgs_sb[t], op=ALU.mult
+            )
+
+        def rewrite(i):
+            nc.vector.tensor_tensor(out=page[i][:].indirect(pos2_sb[:]), in0=looked[i][:], in1=factor[i][:], op=ALU.mult)
+
+        def round_page(i, j0, j1, on_vector):
+            b, t = divmod(i, PACK)
+            g = gain_sb[:, b, t : t + 1]
+            if on_vector:
+                nc.vector.tensor_scalar(
+                    out=b_rows[b][:, t, j0:j1], in0=page[i][:, j0:j1], scalar1=g, scalar2=None, op0=ALU.mult
+                )
+            else:
+                nc.scalar.activation(out=b_rows[b][:, t, j0:j1], in_=page[i][:, j0:j1], func=ACT.Copy, scale=g)
+
+        def weave(b, j0, j1, on_vector):
+            if j0 == 0:
+                b_woven[b] = held.tile([P, S, PACK], BF16, name="b_woven", align_bytes=64)
+            src = b_rows[b][:, :, j0:j1].rearrange("p t j -> p j t")
+            if on_vector:
+                nc.vector.tensor_copy(out=b_woven[b][:, j0:j1, :], in_=src)
+            else:
+                nc.scalar.copy(out=b_woven[b][:, j0:j1, :], in_=src)
+
+        def quantise_page(b, j0, j1):
+            nc.vector.quantize_mx(
+                out=b_codes[b][:, j0:j1].bitcast(FP8X4),
+                scales=b_sc[b][:, j0:j1],
+                in_=b_woven[b][:, j0:j1, :].rearrange("p j t -> p (j t)"),
+            )
+
+        def second_product(b, u):
+            j0, j1 = PIECES[u]
+            for n in range(N // P):
+                if b == 0:
+                    acc[u, n] = psum.tile([P, j1 - j0], F32, name="bank%d" % (4 * (u % 2) + n))
+                nc.tensor.matmul_mx(
+                    out=acc[u, n][:],
+                    lhsT=w4_sb[:, b, 2 * P * n : 2 * P * (n + 1)].bitcast(FP4X4),
+                    lhsT_scale=w4_sc[:, b, P * n : P * (n + 1)],
+                    rhs=b_codes[b][:, j0:j1].bitcast(FP8X4),
+                    rhs_scale=b_sc[b][:, j0:j1],
+                    start=(b == 0),
+                    stop=(b == R_PASSES - 1),
+                )
+
+        def store(u, n0, n1, on_vector):
+            j0, j1 = PIECES[u]
+            result = held.tile([P, n1 - n0, j1 - j0], F32, name="result%d_%d" % (u, n0))
+            for n in range(n0, n1):
+                if on_vector:
+                    nc.vector.tensor_copy(out=result[:, n - n0, :], in_=acc[u, n][:])
+                else:
+                    nc.scalar.copy(out=result[:, n - n0, :], in_=acc[u, n][:])
+            rows = out[n0 * P : n1 * P, j0:j1].rearrange("(n p) j -> p n j", p=P)
+            nc.sync.dma_start(out=rows, in_=result[:])
+
+        first_product(0)
+        first_product(1)
+        for i in range(ROW_TILES):
+            make_factor(i)
+            if i < 2:
+                quantise_w1(1, i + 1, 1 if i == 0 else PACK)
+            if i + 2 < PACK:
+                first_product(i + 2)
+            rewrite(i)
+            if i == 2:
+                for u in range(3):
+                    round_page(u, 0, S, False)
+            if i in (PACK, PACK + 1):
+                j0 = (i - PACK) * BANK
+                weave(0, j0, j0 + BANK // 2, False)
+                weave(0, j0 + BANK // 2, j0 + BANK, False)
+                quantise_page(0, j0, j0 + BANK)
+            if PACK <= i + 2 < ROW_TILES:
+                first_product(i + 2)
+            if i == 5:
+                round_page(4, 0, S, False)
+                second_product(0, 0)
+                second_product(0, 1)
+            if i in (3, 5, 6):
+                round_page(i, 0, S, False)
+        last = ROW_TILES - 1
+        round_page(last, 0, 256, True)
+        weave(1, 0, 256, True)
+        quantise_page(1, 0, 256)
+        second_product(1, 0)
+        round_page(last, 256, 768, False)
+        weave(1, 256, 512, False)
+        weave(1, 512, 768, True)
+        quantise_page(1, 256, 768)
+        second_product(1, 1)
+        round_page(last, 768, S, True)
+        weave(1, 768, S, True)
+        quantise_page(1, 768, S)
+        store(0, 0, 2, False)
+        store(0, 2, 4, False)
+        second_product(0, 2)
+        second_product(1, 2)
+        store(1, 0, 1, False)
+        store(1, 1, 2, False)
+        store(1, 2, 3, True)
+        store(1, 3, 4, True)
+        store(2, 0, 2, False)
+        store(2, 2, 4, True)

@@ -26,7 +26,7 @@ HALVES = S // BANK
 ROW_TILES = R_PASSES * PACK
 QUADRANTS = 4
 PIECES = ((0, 256), (256, 768), (768, 1024))
-SCALAR_SHARE = 64
+SCALAR_SHARE = 32
 
 
 def tile_list_tarnish_bloom_rewrite_kernel(
@@ -123,18 +123,18 @@ def tile_list_tarnish_bloom_rewrite_kernel(
 
         def round_w1(b, a):
             grouped = ring.tile([P, PACK * PASS], BF16, name="w1_bf", align_bytes=64, bufs=3)
-            dst = grouped[:].rearrange("p (t m i) -> p m i t", t=PACK, i=PACK)
-            srcs = [raw[:].rearrange("p i (m t) -> p m i t", t=PACK) for raw in w1_raw[b, a]]
+            dst = grouped[:].rearrange("p (t m e i) -> p m i e t", t=PACK, e=2, i=PACK)
+            srcs = [raw[:].rearrange("p i (m e t) -> p m i e t", e=2, t=PACK) for raw in w1_raw[b, a]]
             if len(srcs) == 2:
-                half = P // 2
+                half = P // 4
                 nc.scalar.copy(out=dst[:, :half], in_=srcs[0])
                 nc.vector.tensor_copy(out=dst[:, half:], in_=srcs[1])
             elif (b, a) == (0, 1):
                 nc.scalar.copy(out=dst[:, :SCALAR_SHARE], in_=srcs[0][:, :SCALAR_SHARE])
                 nc.vector.tensor_copy(out=dst[:, SCALAR_SHARE:], in_=srcs[0][:, SCALAR_SHARE:])
             else:
-                nc.scalar.copy(out=dst[:, : P // 2], in_=srcs[0][:, : P // 2])
-                nc.scalar.copy(out=dst[:, P // 2 :], in_=srcs[0][:, P // 2 :])
+                nc.scalar.copy(out=dst[:, : P // 4], in_=srcs[0][:, : P // 4])
+                nc.scalar.copy(out=dst[:, P // 4 :], in_=srcs[0][:, P // 4 :])
             return grouped
 
         def quantise_w1(b, a, pieces):
@@ -231,11 +231,12 @@ def tile_list_tarnish_bloom_rewrite_kernel(
         def weave(b, j0, j1, on_vector):
             if j0 == 0:
                 b_woven[b] = held.tile([P, S, PACK], BF16, name="b_woven", align_bytes=64)
-            src = b_rows[b][:, :, j0:j1].rearrange("p t j -> p j t")
+            src = b_rows[b][:, :, j0:j1].rearrange("p t (c e) -> p c t e", e=4)
+            dst = b_woven[b][:, j0:j1, :].rearrange("p (c e) t -> p c t e", e=4)
             if on_vector:
-                nc.vector.tensor_copy(out=b_woven[b][:, j0:j1, :], in_=src)
+                nc.vector.tensor_copy(out=dst, in_=src)
             else:
-                nc.scalar.copy(out=b_woven[b][:, j0:j1, :], in_=src)
+                nc.scalar.copy(out=dst, in_=src)
 
         def quantise_page(b, j0, j1):
             nc.vector.quantize_mx(

@@ -1,6 +1,7 @@
 from contextlib import ExitStack
 
 import concourse.mybir as mybir
+from concourse.masks import make_identity
 
 K, H, N, T, S, M = 1536, 1024, 512, 2048, 1024, 512
 FLOPS = 2 * K * H * S + 2 * H * N * S
@@ -26,7 +27,7 @@ HALVES = S // BANK
 ROW_TILES = R_PASSES * PACK
 QUADRANTS = 4
 PIECES = ((0, 256), (256, 768), (768, 1024))
-SCALAR_SHARE = 32
+SCALAR_SHARE = {(0, 1): 32, (0, 2): 22}
 
 
 def tile_list_tarnish_bloom_rewrite_kernel(
@@ -85,18 +86,32 @@ def tile_list_tarnish_bloom_rewrite_kernel(
             for t in range(t0, t1):
                 tint_sb[PACK * b + t] = tile[:, t - t0, :]
 
-        def load_wgs(t0, t1):
-            rows = wgs.rearrange("(q t) m -> q t m", t=PACK)
-            tile = held.tile([P, t1 - t0, M], F32, name="wgs%d" % t0)
-            for quad in (0, 2, 1, 3):
-                nc.sync.dma_start(out=tile[32 * quad : 32 * quad + 32, :, :], in_=rows[:, t0:t1, :])
-            for t in range(t0, t1):
-                wgs_sb[t] = tile[:, t - t0, :]
+        def deal_wgs():
+            rows = held.tile([P, M], F32, name="wgs_rows")
+            nc.sync.dma_start(out=rows[:], in_=wgs)
+            identity = held.tile([P, P], F32, name="identity")
+            make_identity(nc, identity[:])
+            turned = psum.tile([P, M // P, P], F32, name="bank7")
+            for u in range(M // P):
+                nc.tensor.transpose(turned[:, u, :], rows[:, u * P : (u + 1) * P], identity[:])
+            dealt = ring.tile([P, M // P, PACK, P], F32, name="w1_raw", bufs=5)
+            for quad in range(QUADRANTS):
+                nc.scalar.copy(
+                    out=dealt[:, :, :, 32 * quad : 32 * quad + 32],
+                    in_=turned[:].rearrange("p u (q t) -> p u t q", t=PACK),
+                )
+            for t in range(PACK):
+                back = psum.tile([P, M], F32, name="bank%d" % t)
+                for u in range(M // P):
+                    nc.tensor.transpose(back[:, u * P : (u + 1) * P], dealt[:, u, t, :], identity[:])
+                wgs_sb[t] = held.tile([P, M], F32, name="wgs%d" % t)
+                nc.scalar.copy(out=wgs_sb[t][:], in_=back[:])
 
         nc.sync.dma_start(offs_sb[:], offs)
+        deal_wgs()
         load_tab(0)
-        nc.sync.dma_start(pos1_sb[:], pos1)
         nc.sync.dma_start(pos2_sb[:], pos2)
+        nc.sync.dma_start(pos1_sb[:], pos1)
         for quad in range(QUADRANTS):
             nc.sync.dma_start(
                 out=tab_sc[32 * quad : 32 * quad + 4 * K_PASSES, :].bitcast(I32),
@@ -106,15 +121,14 @@ def tile_list_tarnish_bloom_rewrite_kernel(
         load_tab(1)
         load_tab(2)
         load_w1(0, 1, 1)
-        load_w1(0, 2, 2)
+        load_w1(0, 2, 1)
         nc.sync.dma_start(out=skip_sb[:], in_=skip.rearrange("(b p t) -> p b t", p=P, t=PACK))
         load_w1(1, 0, 1)
         load_tint(0, 0, 1)
-        load_wgs(0, 1)
+        load_tint(0, 1, 3)
         load_w1(1, 1, 1)
-        load_tint(0, 1, PACK)
-        load_wgs(1, PACK)
         load_w1(1, 2, 1)
+        load_tint(0, 3, PACK)
         nc.sync.dma_start(out=gain_sb[:], in_=gain.rearrange("(b p t) -> p b t", p=P, t=PACK))
         load_tint(1, 0, PACK)
 
@@ -124,17 +138,13 @@ def tile_list_tarnish_bloom_rewrite_kernel(
         def round_w1(b, a):
             grouped = ring.tile([P, PACK * PASS], BF16, name="w1_bf", align_bytes=64, bufs=3)
             dst = grouped[:].rearrange("p (t m e i) -> p m i e t", t=PACK, e=2, i=PACK)
-            srcs = [raw[:].rearrange("p i (m e t) -> p m i e t", e=2, t=PACK) for raw in w1_raw[b, a]]
-            if len(srcs) == 2:
-                half = P // 4
-                nc.scalar.copy(out=dst[:, :half], in_=srcs[0])
-                nc.vector.tensor_copy(out=dst[:, half:], in_=srcs[1])
-            elif (b, a) == (0, 1):
-                nc.scalar.copy(out=dst[:, :SCALAR_SHARE], in_=srcs[0][:, :SCALAR_SHARE])
-                nc.vector.tensor_copy(out=dst[:, SCALAR_SHARE:], in_=srcs[0][:, SCALAR_SHARE:])
+            src = w1_raw[b, a][0][:].rearrange("p i (m e t) -> p m i e t", e=2, t=PACK)
+            cut = SCALAR_SHARE.get((b, a), P // 4)
+            nc.scalar.copy(out=dst[:, :cut], in_=src[:, :cut])
+            if (b, a) in SCALAR_SHARE:
+                nc.vector.tensor_copy(out=dst[:, cut:], in_=src[:, cut:])
             else:
-                nc.scalar.copy(out=dst[:, : P // 4], in_=srcs[0][:, : P // 4])
-                nc.scalar.copy(out=dst[:, P // 4 :], in_=srcs[0][:, P // 4 :])
+                nc.scalar.copy(out=dst[:, cut:], in_=src[:, cut:])
             return grouped
 
         def quantise_w1(b, a, pieces):
@@ -212,7 +222,7 @@ def tile_list_tarnish_bloom_rewrite_kernel(
             t = i % PACK
             factor[i] = ring.tile([P, M], F32, name="factor", bufs=3)
             nc.gpsimd.tensor_tensor(
-                out=factor[i][:], in0=tint_sb[i], in1=wgs_sb[t], op=ALU.mult
+                out=factor[i][:], in0=tint_sb[i], in1=wgs_sb[t][:], op=ALU.mult
             )
 
         def rewrite(i):
@@ -301,16 +311,17 @@ def tile_list_tarnish_bloom_rewrite_kernel(
         weave(1, 0, 256, True)
         quantise_page(1, 0, 256)
         second_product(1, 0)
-        round_page(last, 256, 768, False)
+        round_page(last, 256, 512, False)
         weave(1, 256, 512, False)
+        round_page(last, 512, 768, True)
         weave(1, 512, 768, True)
         quantise_page(1, 256, 768)
         second_product(1, 1)
-        round_page(last, 768, S, True)
+        store(0, 0, 2, False)
+        round_page(last, 768, S, False)
+        store(0, 2, 4, False)
         weave(1, 768, S, True)
         quantise_page(1, 768, S)
-        store(0, 0, 2, False)
-        store(0, 2, 4, False)
         second_product(0, 2)
         second_product(1, 2)
         store(1, 0, 1, False)

@@ -22,12 +22,23 @@ PACK = 4
 PASS = P * PACK
 K_PASSES = K // PASS
 R_PASSES = H // PASS
+ROW_TILES = R_PASSES * PACK
 BANK = 512
 HALVES = S // BANK
-ROW_TILES = R_PASSES * PACK
+N_TILES = N // P
 QUADRANTS = 4
-PIECES = ((0, 256), (256, 768), (768, 1024))
-SCALAR_SHARE = {(0, 1): 32, (0, 2): 22}
+QUADRANT = P // QUADRANTS
+SCALE_ROWS = 4
+LIST_GROUP = 16
+QUARTER = S // 4
+
+W1_STEPS = P // 2
+SCALAR_STEPS = {(0, 1): W1_STEPS // 2, (0, 2): 22}
+PIECES = ((0, QUARTER), (QUARTER, 3 * QUARTER), (3 * QUARTER, S))
+
+RAW_BUFS = 5
+LOOK_BUFS = 4
+PAGE_BUFS = 5
 
 
 def tile_list_tarnish_bloom_rewrite_kernel(
@@ -39,52 +50,42 @@ def tile_list_tarnish_bloom_rewrite_kernel(
         ring = ctx.enter_context(tc.tile_pool(name="ring", bufs=3))
         psum = ctx.enter_context(tc.psum_pool(name="psum", bufs=1))
 
-        offs_sb = held.tile([P, S // 16], U16, name="offs_sb")
-        pos1_sb = held.tile([P, M // 16], U16, name="pos1_sb")
-        pos2_sb = held.tile([P, M // 16], U16, name="pos2_sb")
+        offs_sb = held.tile([P, S // LIST_GROUP], U16, name="offs_sb")
+        pos1_sb = held.tile([P, M // LIST_GROUP], U16, name="pos1_sb")
+        pos2_sb = held.tile([P, M // LIST_GROUP], U16, name="pos2_sb")
         tab_sb = [held.tile([P, T], I32, name="tab%d" % a, align_bytes=64) for a in range(K_PASSES)]
         tab_sc = held.tile([P, T], U8, name="tab_sc", align_bytes=64)
         v_words = [held.tile([P, S], U32, name="v_words%d" % a, align_bytes=64) for a in range(K_PASSES)]
         v_sc = held.tile([P, S], U8, name="v_sc", align_bytes=64)
         w1_codes = {}
         w1_sc = {}
-        w1_raw = {}
         for b in range(R_PASSES):
             for a in range(K_PASSES):
                 w1_codes[b, a] = held.tile([P, PASS], U32, name="w1_codes%d_%d" % (b, a), align_bytes=64)
                 w1_sc[b, a] = held.tile([P, PASS], U8, name="w1_sc%d_%d" % (b, a), align_bytes=64)
-        tint_sb = {}
-        wgs_sb = {}
         skip_sb = held.tile([P, R_PASSES, PACK], F32, name="skip_sb")
         gain_sb = held.tile([P, R_PASSES, PACK], F32, name="gain_sb")
         w4_sb = held.tile([P, R_PASSES, 2 * N], U8, name="w4_sb", align_bytes=64)
         w4_sc = held.tile([P, R_PASSES, N], U8, name="w4_sc", align_bytes=64)
         b_codes = [held.tile([P, S], U32, name="b_codes%d" % b, align_bytes=64) for b in range(R_PASSES)]
         b_sc = [held.tile([P, S], U8, name="b_sc%d" % b, align_bytes=64) for b in range(R_PASSES)]
-        b_woven = [None] * R_PASSES
         b_rows = [held.tile([P, PACK, S], BF16, name="b_rows%d" % b, align_bytes=64) for b in range(R_PASSES)]
-
-        nc.gpsimd.memset(tab_sc[:].bitcast(U32), 0)
+        w1_raw, tint_sb, wgs_sb, looked, page, factor, b_woven, acc = {}, {}, {}, {}, {}, {}, {}, {}
 
         def load_tab(a):
             nc.sync.dma_start(out=tab_sb[a][:], in_=tab_words[a].rearrange("p t i -> p (t i)").bitcast(I32))
 
-        def load_w1(b, a, pieces):
-            width = PASS // pieces
-            w1_raw[b, a] = []
-            for u in range(pieces):
-                raw = ring.tile([P, PACK, width], F32, name="w1_raw", bufs=5)
-                c0 = b * PASS + u * width
-                rows = w1[a * PASS : (a + 1) * PASS, c0 : c0 + width]
-                nc.sync.dma_start(out=raw[:], in_=rows.rearrange("(p i) c -> p i c", i=PACK))
-                w1_raw[b, a].append(raw)
+        def load_w1(b, a):
+            w1_raw[b, a] = ring.tile([P, PACK, PASS], F32, name="w1_raw", bufs=RAW_BUFS)
+            rows = w1[a * PASS : (a + 1) * PASS, b * PASS : (b + 1) * PASS]
+            nc.sync.dma_start(out=w1_raw[b, a][:], in_=rows.rearrange("(p i) c -> p i c", i=PACK))
 
         def load_tint(b, t0, t1):
             rows = tint[b * PASS : (b + 1) * PASS, :].rearrange("(p t) m -> p t m", t=PACK)
-            tile = held.tile([P, t1 - t0, M], F32, name="tint%d_%d" % (b, t0))
-            nc.sync.dma_start(out=tile[:], in_=rows[:, t0:t1, :])
+            loaded = held.tile([P, t1 - t0, M], F32, name="tint%d_%d" % (b, t0))
+            nc.sync.dma_start(out=loaded[:], in_=rows[:, t0:t1, :])
             for t in range(t0, t1):
-                tint_sb[PACK * b + t] = tile[:, t - t0, :]
+                tint_sb[PACK * b + t] = loaded[:, t - t0, :]
 
         def deal_wgs():
             rows = held.tile([P, M], F32, name="wgs_rows")
@@ -94,10 +95,10 @@ def tile_list_tarnish_bloom_rewrite_kernel(
             turned = psum.tile([P, M // P, P], F32, name="bank7")
             for u in range(M // P):
                 nc.tensor.transpose(turned[:, u, :], rows[:, u * P : (u + 1) * P], identity[:])
-            dealt = ring.tile([P, M // P, PACK, P], F32, name="w1_raw", bufs=5)
+            dealt = ring.tile([P, M // P, PACK, P], F32, name="w1_raw", bufs=RAW_BUFS)
             for quad in range(QUADRANTS):
                 nc.scalar.copy(
-                    out=dealt[:, :, :, 32 * quad : 32 * quad + 32],
+                    out=dealt[:, :, :, QUADRANT * quad : QUADRANT * (quad + 1)],
                     in_=turned[:].rearrange("p u (q t) -> p u t q", t=PACK),
                 )
             for t in range(PACK):
@@ -107,87 +108,35 @@ def tile_list_tarnish_bloom_rewrite_kernel(
                 wgs_sb[t] = held.tile([P, M], F32, name="wgs%d" % t)
                 nc.scalar.copy(out=wgs_sb[t][:], in_=back[:])
 
-        nc.sync.dma_start(offs_sb[:], offs)
-        deal_wgs()
-        load_tab(0)
-        nc.sync.dma_start(pos2_sb[:], pos2)
-        nc.sync.dma_start(pos1_sb[:], pos1)
-        for quad in range(QUADRANTS):
-            nc.sync.dma_start(
-                out=tab_sc[32 * quad : 32 * quad + 4 * K_PASSES, :].bitcast(I32),
-                in_=tab_scales[:, 4 * quad : 4 * quad + 4, :].bitcast(I32),
-            )
-        load_w1(0, 0, 1)
-        load_tab(1)
-        load_tab(2)
-        load_w1(0, 1, 1)
-        load_w1(0, 2, 1)
-        nc.sync.dma_start(out=skip_sb[:], in_=skip.rearrange("(b p t) -> p b t", p=P, t=PACK))
-        load_w1(1, 0, 1)
-        load_tint(0, 0, 1)
-        load_tint(0, 1, 3)
-        load_w1(1, 1, 1)
-        load_w1(1, 2, 1)
-        load_tint(0, 3, PACK)
-        nc.sync.dma_start(out=gain_sb[:], in_=gain.rearrange("(b p t) -> p b t", p=P, t=PACK))
-        load_tint(1, 0, PACK)
-
         def gather_words(a):
             nc.vector.tensor_copy(out=v_words[a][:], in_=tab_sb[a][:].bitcast(U32).indirect(offs_sb[:]))
 
-        def round_w1(b, a):
-            grouped = ring.tile([P, PACK * PASS], BF16, name="w1_bf", align_bytes=64, bufs=3)
-            dst = grouped[:].rearrange("p (t m e i) -> p m i e t", t=PACK, e=2, i=PACK)
-            src = w1_raw[b, a][0][:].rearrange("p i (m e t) -> p m i e t", e=2, t=PACK)
-            cut = SCALAR_SHARE.get((b, a), P // 4)
+        def quantise_w1(b, a, calls):
+            rounded = ring.tile([P, PACK * PASS], BF16, name="w1_bf", align_bytes=64)
+            dst = rounded[:].rearrange("p (t m e i) -> p m i e t", t=PACK, e=2, i=PACK)
+            src = w1_raw[b, a][:].rearrange("p i (m e t) -> p m i e t", e=2, t=PACK)
+            cut = SCALAR_STEPS.get((b, a), W1_STEPS // 2)
             nc.scalar.copy(out=dst[:, :cut], in_=src[:, :cut])
-            if (b, a) in SCALAR_SHARE:
+            if (b, a) in SCALAR_STEPS:
                 nc.vector.tensor_copy(out=dst[:, cut:], in_=src[:, cut:])
             else:
                 nc.scalar.copy(out=dst[:, cut:], in_=src[:, cut:])
-            return grouped
-
-        def quantise_w1(b, a, pieces):
-            grouped = round_w1(b, a)
-            width = PASS // pieces
-            for u in range(pieces):
+            width = PASS // calls
+            for u in range(calls):
                 cols = slice(u * width, (u + 1) * width)
                 nc.vector.quantize_mx(
                     out=w1_codes[b, a][:, cols].bitcast(FP8X4),
                     scales=w1_sc[b, a][:, cols],
-                    in_=grouped[:, PACK * u * width : PACK * (u + 1) * width],
+                    in_=rounded[:, PACK * u * width : PACK * (u + 1) * width],
                 )
 
-        gather_words(0)
-        nc.vector.tensor_copy(out=v_sc[:], in_=tab_sc[:].indirect(offs_sb[:]))
-        gather_words(1)
-        quantise_w1(0, 0, 1)
-        gather_words(2)
-        quantise_w1(0, 1, 1)
-        quantise_w1(0, 2, PACK)
-
-        quantise_w1(1, 0, 1)
-        nc.gpsimd.memset(w4_sc[:].rearrange("p b n -> p (b n)").bitcast(U32), 0)
-        for b in range(R_PASSES):
-            nc.sync.dma_start(out=w4_sb[:, b, :].bitcast(I32), in_=w4_words[b].bitcast(I32))
-        for quad in range(QUADRANTS):
-            nc.sync.dma_start(
-                out=w4_sc[32 * quad : 32 * quad + 4, :, :].bitcast(I32),
-                in_=w4_scales[:, 4 * quad : 4 * quad + 4, :].rearrange("b r n -> r b n").bitcast(I32),
-            )
-
-        h_sb = {}
-        looked = {}
-        page = {}
-        acc = {}
-
-        def first_product(i):
+        def look(i):
             b, t = divmod(i, PACK)
             cols = slice(t * P, (t + 1) * P)
-            h_sb[i] = ring.tile([P, S], F32, name="h_sb")
+            h_sb = ring.tile([P, S], F32, name="h_sb")
             tops = ring.tile([P, HALVES], F32, name="tops")
             neg_top = ring.tile([P, 1], F32, name="neg_top")
-            banks = [psum.tile([P, BANK], F32, name="bank%d" % (HALVES * (i % PACK) + c)) for c in range(HALVES)]
+            banks = [psum.tile([P, BANK], F32, name="bank%d" % (HALVES * (i % 2) + c)) for c in range(HALVES)]
             for a in range(K_PASSES):
                 for c in range(HALVES):
                     js = slice(c * BANK, (c + 1) * BANK)
@@ -196,53 +145,48 @@ def tile_list_tarnish_bloom_rewrite_kernel(
                         lhsT=w1_codes[b, a][:, cols].bitcast(FP8X4),
                         lhsT_scale=w1_sc[b, a][:, cols],
                         rhs=v_words[a][:, js].bitcast(FP8X4),
-                        rhs_scale=v_sc[4 * a : P, js],
+                        rhs_scale=v_sc[SCALE_ROWS * a : P, js],
                         start=(a == 0),
                         stop=(a == K_PASSES - 1),
                     )
             for c in range(HALVES):
                 nc.vector.tensor_scalar(
-                    out=h_sb[i][:, c * BANK : (c + 1) * BANK],
+                    out=h_sb[:, c * BANK : (c + 1) * BANK],
                     in0=banks[c][:],
                     scalar1=1.0,
-                    scalar2=tops[:, 0:1] if c else None,
+                    scalar2=tops[:, c - 1 : c] if c else None,
                     op0=ALU.mult,
                     op1=ALU.max,
                     accum_out=tops[:, c : c + 1],
                 )
-            nc.scalar.activation(out=neg_top[:], in_=tops[:, 1:2], func=ACT.Copy, scale=-1.0)
-            looked[i] = ring.tile([P, M], F32, name="looked", bufs=4)
-            nc.scalar.activation(out=looked[i][:], in_=h_sb[i][:].indirect(pos1_sb[:]), func=ACT.Exp, bias=neg_top[:])
-            page[i] = ring.tile([P, S], F32, name="page", bufs=5)
-            nc.scalar.activation(out=page[i][:], in_=h_sb[i][:], func=ACT.Copy, scale=skip_sb[:, b, t : t + 1])
-
-        factor = {}
+            nc.scalar.activation(out=neg_top[:], in_=tops[:, HALVES - 1 : HALVES], func=ACT.Copy, scale=-1.0)
+            looked[i] = ring.tile([P, M], F32, name="looked", bufs=LOOK_BUFS)
+            nc.scalar.activation(out=looked[i][:], in_=h_sb[:].indirect(pos1_sb[:]), func=ACT.Exp, bias=neg_top[:])
+            page[i] = ring.tile([P, S], F32, name="page", bufs=PAGE_BUFS)
+            nc.scalar.activation(out=page[i][:], in_=h_sb[:], func=ACT.Copy, scale=skip_sb[:, b, t : t + 1])
 
         def make_factor(i):
-            t = i % PACK
-            factor[i] = ring.tile([P, M], F32, name="factor", bufs=3)
-            nc.gpsimd.tensor_tensor(
-                out=factor[i][:], in0=tint_sb[i], in1=wgs_sb[t][:], op=ALU.mult
-            )
+            factor[i] = ring.tile([P, M], F32, name="factor")
+            nc.gpsimd.tensor_tensor(out=factor[i][:], in0=tint_sb[i], in1=wgs_sb[i % PACK][:], op=ALU.mult)
 
         def rewrite(i):
             nc.vector.tensor_tensor(out=page[i][:].indirect(pos2_sb[:]), in0=looked[i][:], in1=factor[i][:], op=ALU.mult)
 
-        def round_page(i, j0, j1, on_vector):
+        def round_page(i, j0=0, j1=S, on_vector=False):
             b, t = divmod(i, PACK)
-            g = gain_sb[:, b, t : t + 1]
+            row_gain = gain_sb[:, b, t : t + 1]
             if on_vector:
                 nc.vector.tensor_scalar(
-                    out=b_rows[b][:, t, j0:j1], in0=page[i][:, j0:j1], scalar1=g, scalar2=None, op0=ALU.mult
+                    out=b_rows[b][:, t, j0:j1], in0=page[i][:, j0:j1], scalar1=row_gain, scalar2=None, op0=ALU.mult
                 )
             else:
-                nc.scalar.activation(out=b_rows[b][:, t, j0:j1], in_=page[i][:, j0:j1], func=ACT.Copy, scale=g)
+                nc.scalar.activation(out=b_rows[b][:, t, j0:j1], in_=page[i][:, j0:j1], func=ACT.Copy, scale=row_gain)
 
-        def weave(b, j0, j1, on_vector):
+        def weave(b, j0, on_vector=False):
             if j0 == 0:
                 b_woven[b] = held.tile([P, S, PACK], BF16, name="b_woven", align_bytes=64)
-            src = b_rows[b][:, :, j0:j1].rearrange("p t (c e) -> p c t e", e=4)
-            dst = b_woven[b][:, j0:j1, :].rearrange("p (c e) t -> p c t e", e=4)
+            src = b_rows[b][:, :, j0 : j0 + QUARTER].rearrange("p t (c e) -> p c t e", e=4)
+            dst = b_woven[b][:, j0 : j0 + QUARTER, :].rearrange("p (c e) t -> p c t e", e=4)
             if on_vector:
                 nc.vector.tensor_copy(out=dst, in_=src)
             else:
@@ -257,9 +201,9 @@ def tile_list_tarnish_bloom_rewrite_kernel(
 
         def second_product(b, u):
             j0, j1 = PIECES[u]
-            for n in range(N // P):
+            for n in range(N_TILES):
                 if b == 0:
-                    acc[u, n] = psum.tile([P, j1 - j0], F32, name="bank%d" % (4 * (u % 2) + n))
+                    acc[u, n] = psum.tile([P, j1 - j0], F32, name="bank%d" % (N_TILES * (1 - u % 2) + n))
                 nc.tensor.matmul_mx(
                     out=acc[u, n][:],
                     lhsT=w4_sb[:, b, 2 * P * n : 2 * P * (n + 1)].bitcast(FP4X4),
@@ -270,7 +214,7 @@ def tile_list_tarnish_bloom_rewrite_kernel(
                     stop=(b == R_PASSES - 1),
                 )
 
-        def store(u, n0, n1, on_vector):
+        def store(u, n0, n1, on_vector=False):
             j0, j1 = PIECES[u]
             result = held.tile([P, n1 - n0, j1 - j0], F32, name="result%d_%d" % (u, n0))
             for n in range(n0, n1):
@@ -278,55 +222,105 @@ def tile_list_tarnish_bloom_rewrite_kernel(
                     nc.vector.tensor_copy(out=result[:, n - n0, :], in_=acc[u, n][:])
                 else:
                     nc.scalar.copy(out=result[:, n - n0, :], in_=acc[u, n][:])
-            rows = out[n0 * P : n1 * P, j0:j1].rearrange("(n p) j -> p n j", p=P)
-            nc.sync.dma_start(out=rows, in_=result[:])
+            nc.sync.dma_start(out=out[n0 * P : n1 * P, j0:j1].rearrange("(n p) j -> p n j", p=P), in_=result[:])
 
-        first_product(0)
-        first_product(1)
-        for i in range(ROW_TILES):
+        nc.gpsimd.memset(tab_sc[:].bitcast(U32), 0)
+
+        nc.sync.dma_start(offs_sb[:], offs)
+        deal_wgs()
+        load_tab(0)
+        nc.sync.dma_start(pos2_sb[:], pos2)
+        nc.sync.dma_start(pos1_sb[:], pos1)
+        for quad in range(QUADRANTS):
+            nc.sync.dma_start(
+                out=tab_sc[QUADRANT * quad : QUADRANT * quad + SCALE_ROWS * K_PASSES, :].bitcast(I32),
+                in_=tab_scales[:, SCALE_ROWS * quad : SCALE_ROWS * (quad + 1), :].bitcast(I32),
+            )
+        load_w1(0, 0)
+        for a in range(1, K_PASSES):
+            load_tab(a)
+            load_w1(0, a)
+        nc.sync.dma_start(out=skip_sb[:], in_=skip.rearrange("(b p t) -> p b t", p=P, t=PACK))
+        load_w1(1, 0)
+        load_tint(0, 0, 1)
+        load_tint(0, 1, PACK - 1)
+        for a in range(1, K_PASSES):
+            load_w1(1, a)
+        load_tint(0, PACK - 1, PACK)
+        nc.sync.dma_start(out=gain_sb[:], in_=gain.rearrange("(b p t) -> p b t", p=P, t=PACK))
+        load_tint(1, 0, PACK)
+
+        gather_words(0)
+        nc.vector.tensor_copy(out=v_sc[:], in_=tab_sc[:].indirect(offs_sb[:]))
+        gather_words(1)
+        quantise_w1(0, 0, 1)
+        quantise_w1(0, 1, 1)
+        gather_words(2)
+        quantise_w1(0, 2, PACK)
+        quantise_w1(1, 0, 1)
+
+        nc.gpsimd.memset(w4_sc[:].rearrange("p b n -> p (b n)").bitcast(U32), 0)
+        for b in range(R_PASSES):
+            nc.sync.dma_start(out=w4_sb[:, b, :].bitcast(I32), in_=w4_words[b].bitcast(I32))
+        for quad in range(QUADRANTS):
+            nc.sync.dma_start(
+                out=w4_sc[QUADRANT * quad : QUADRANT * quad + SCALE_ROWS, :, :].bitcast(I32),
+                in_=w4_scales[:, SCALE_ROWS * quad : SCALE_ROWS * (quad + 1), :].rearrange("b r n -> r b n").bitcast(I32),
+            )
+
+        look(0)
+        look(1)
+        for i in range(2):
             make_factor(i)
-            if i < 2:
-                quantise_w1(1, i + 1, 1 if i == 0 else PACK)
-            if i + 2 < PACK:
-                first_product(i + 2)
+            quantise_w1(1, i + 1, PACK if i + 2 == K_PASSES else 1)
+            look(i + 2)
             rewrite(i)
-            if i == 2:
-                for u in range(3):
-                    round_page(u, 0, S, False)
-            if i in (PACK, PACK + 1):
-                j0 = (i - PACK) * BANK
-                weave(0, j0, j0 + BANK // 2, False)
-                weave(0, j0 + BANK // 2, j0 + BANK, False)
-                quantise_page(0, j0, j0 + BANK)
-            if PACK <= i + 2 < ROW_TILES:
-                first_product(i + 2)
-            if i == 5:
-                round_page(4, 0, S, False)
-                second_product(0, 0)
-                second_product(0, 1)
-            if i in (3, 5, 6):
-                round_page(i, 0, S, False)
+        make_factor(2)
+        rewrite(2)
+        for i in range(3):
+            round_page(i)
+        look(4)
+        make_factor(3)
+        rewrite(3)
+        look(5)
+        round_page(3)
+
+        for c in range(HALVES):
+            make_factor(PACK + c)
+            rewrite(PACK + c)
+            weave(0, c * BANK)
+            weave(0, c * BANK + QUARTER)
+            quantise_page(0, c * BANK, (c + 1) * BANK)
+            look(PACK + c + 2)
+        round_page(4)
+        second_product(0, 0)
+        second_product(0, 1)
+        round_page(5)
         last = ROW_TILES - 1
-        round_page(last, 0, 256, True)
-        weave(1, 0, 256, True)
-        quantise_page(1, 0, 256)
+        make_factor(last - 1)
+        rewrite(last - 1)
+        round_page(last - 1)
+        make_factor(last)
+        rewrite(last)
+
+        round_page(last, 0, QUARTER, on_vector=True)
+        weave(1, 0, on_vector=True)
+        quantise_page(1, *PIECES[0])
         second_product(1, 0)
-        round_page(last, 256, 512, False)
-        weave(1, 256, 512, False)
-        round_page(last, 512, 768, True)
-        weave(1, 512, 768, True)
-        quantise_page(1, 256, 768)
+        round_page(last, QUARTER, 2 * QUARTER)
+        weave(1, QUARTER)
+        round_page(last, 2 * QUARTER, 3 * QUARTER, on_vector=True)
+        weave(1, 2 * QUARTER, on_vector=True)
+        quantise_page(1, *PIECES[1])
         second_product(1, 1)
-        store(0, 0, 2, False)
-        round_page(last, 768, S, False)
-        store(0, 2, 4, False)
-        weave(1, 768, S, True)
-        quantise_page(1, 768, S)
+        store(0, 0, N_TILES // 2)
+        round_page(last, 3 * QUARTER, S)
+        store(0, N_TILES // 2, N_TILES)
+        weave(1, 3 * QUARTER, on_vector=True)
+        quantise_page(1, *PIECES[2])
         second_product(0, 2)
         second_product(1, 2)
-        store(1, 0, 1, False)
-        store(1, 1, 2, False)
-        store(1, 2, 3, True)
-        store(1, 3, 4, True)
-        store(2, 0, 2, False)
-        store(2, 2, 4, True)
+        for n in range(N_TILES):
+            store(1, n, n + 1, on_vector=(n >= N_TILES // 2))
+        store(2, 0, N_TILES // 2)
+        store(2, N_TILES // 2, N_TILES, on_vector=True)

from contextlib import ExitStack

import concourse.mybir as mybir
from concourse.masks import make_identity

K, H, N, T, S, M = 1536, 1024, 512, 2048, 1024, 512
FLOPS = 2 * K * H * S + 2 * H * N * S

F32 = mybir.dt.float32
BF16 = mybir.dt.bfloat16
I32 = mybir.dt.int32
U32 = mybir.dt.uint32
U16 = mybir.dt.uint16
U8 = mybir.dt.uint8
FP8X4 = mybir.dt.float8_e4m3fn_x4
FP4X4 = mybir.dt.float4_e2m1fn_x4
ALU = mybir.AluOpType
ACT = mybir.ActivationFunctionType

P = 128
PACK = 4
PASS = P * PACK
K_PASSES = K // PASS
R_PASSES = H // PASS
ROW_TILES = R_PASSES * PACK
BANK = 512
HALVES = S // BANK
N_TILES = N // P
QUADRANTS = 4
QUADRANT = P // QUADRANTS
SCALE_ROWS = 4
LIST_GROUP = 16
QUARTER = S // 4

W1_STEPS = P // 2
SCALAR_STEPS = {(0, 1): W1_STEPS // 2, (0, 2): 22}
PIECES = ((0, QUARTER), (QUARTER, 3 * QUARTER), (3 * QUARTER, S))

RAW_BUFS = 5
LOOK_BUFS = 4
PAGE_BUFS = 5


def tile_list_tarnish_bloom_rewrite_kernel(
    tc, tab_words, tab_scales, offs, pos1, pos2, w1, tint, skip, wgs, gain, w4_words, w4_scales, out
):
    nc = tc.nc
    with ExitStack() as ctx:
        held = ctx.enter_context(tc.tile_pool(name="held", bufs=1))
        ring = ctx.enter_context(tc.tile_pool(name="ring", bufs=3))
        psum = ctx.enter_context(tc.psum_pool(name="psum", bufs=1))

        offs_sb = held.tile([P, S // LIST_GROUP], U16, name="offs_sb")
        pos1_sb = held.tile([P, M // LIST_GROUP], U16, name="pos1_sb")
        pos2_sb = held.tile([P, M // LIST_GROUP], U16, name="pos2_sb")
        tab_sb = [held.tile([P, T], I32, name="tab%d" % a, align_bytes=64) for a in range(K_PASSES)]
        tab_sc = held.tile([P, T], U8, name="tab_sc", align_bytes=64)
        v_words = [held.tile([P, S], U32, name="v_words%d" % a, align_bytes=64) for a in range(K_PASSES)]
        v_sc = held.tile([P, S], U8, name="v_sc", align_bytes=64)
        w1_codes = {}
        w1_sc = {}
        for b in range(R_PASSES):
            for a in range(K_PASSES):
                w1_codes[b, a] = held.tile([P, PASS], U32, name="w1_codes%d_%d" % (b, a), align_bytes=64)
                w1_sc[b, a] = held.tile([P, PASS], U8, name="w1_sc%d_%d" % (b, a), align_bytes=64)
        skip_sb = held.tile([P, R_PASSES, PACK], F32, name="skip_sb")
        gain_sb = held.tile([P, R_PASSES, PACK], F32, name="gain_sb")
        w4_sb = held.tile([P, R_PASSES, 2 * N], U8, name="w4_sb", align_bytes=64)
        w4_sc = held.tile([P, R_PASSES, N], U8, name="w4_sc", align_bytes=64)
        b_codes = [held.tile([P, S], U32, name="b_codes%d" % b, align_bytes=64) for b in range(R_PASSES)]
        b_sc = [held.tile([P, S], U8, name="b_sc%d" % b, align_bytes=64) for b in range(R_PASSES)]
        b_rows = [held.tile([P, PACK, S], BF16, name="b_rows%d" % b, align_bytes=64) for b in range(R_PASSES)]
        w1_raw, tint_sb, wgs_sb, looked, page, factor, b_woven, acc = {}, {}, {}, {}, {}, {}, {}, {}

        def load_tab(a):
            nc.sync.dma_start(out=tab_sb[a][:], in_=tab_words[a].rearrange("p t i -> p (t i)").bitcast(I32))

        def load_w1(b, a):
            w1_raw[b, a] = ring.tile([P, PACK, PASS], F32, name="w1_raw", bufs=RAW_BUFS)
            rows = w1[a * PASS : (a + 1) * PASS, b * PASS : (b + 1) * PASS]
            nc.sync.dma_start(out=w1_raw[b, a][:], in_=rows.rearrange("(p i) c -> p i c", i=PACK))

        def load_tint(b, t0, t1):
            rows = tint[b * PASS : (b + 1) * PASS, :].rearrange("(p t) m -> p t m", t=PACK)
            loaded = held.tile([P, t1 - t0, M], F32, name="tint%d_%d" % (b, t0))
            nc.sync.dma_start(out=loaded[:], in_=rows[:, t0:t1, :])
            for t in range(t0, t1):
                tint_sb[PACK * b + t] = loaded[:, t - t0, :]

        def deal_wgs():
            rows = held.tile([P, M], F32, name="wgs_rows")
            nc.sync.dma_start(out=rows[:], in_=wgs)
            identity = held.tile([P, P], F32, name="identity")
            make_identity(nc, identity[:])
            turned = psum.tile([P, M // P, P], F32, name="bank7")
            for u in range(M // P):
                nc.tensor.transpose(turned[:, u, :], rows[:, u * P : (u + 1) * P], identity[:])
            dealt = ring.tile([P, M // P, PACK, P], F32, name="w1_raw", bufs=RAW_BUFS)
            for quad in range(QUADRANTS):
                nc.scalar.copy(
                    out=dealt[:, :, :, QUADRANT * quad : QUADRANT * (quad + 1)],
                    in_=turned[:].rearrange("p u (q t) -> p u t q", t=PACK),
                )
            for t in range(PACK):
                back = psum.tile([P, M], F32, name="bank%d" % t)
                for u in range(M // P):
                    nc.tensor.transpose(back[:, u * P : (u + 1) * P], dealt[:, u, t, :], identity[:])
                wgs_sb[t] = held.tile([P, M], F32, name="wgs%d" % t)
                nc.scalar.copy(out=wgs_sb[t][:], in_=back[:])

        def gather_words(a):
            nc.vector.tensor_copy(out=v_words[a][:], in_=tab_sb[a][:].bitcast(U32).indirect(offs_sb[:]))

        def quantise_w1(b, a, calls):
            rounded = ring.tile([P, PACK * PASS], BF16, name="w1_bf", align_bytes=64)
            dst = rounded[:].rearrange("p (t m e i) -> p m i e t", t=PACK, e=2, i=PACK)
            src = w1_raw[b, a][:].rearrange("p i (m e t) -> p m i e t", e=2, t=PACK)
            cut = SCALAR_STEPS.get((b, a), W1_STEPS // 2)
            nc.scalar.copy(out=dst[:, :cut], in_=src[:, :cut])
            if (b, a) in SCALAR_STEPS:
                nc.vector.tensor_copy(out=dst[:, cut:], in_=src[:, cut:])
            else:
                nc.scalar.copy(out=dst[:, cut:], in_=src[:, cut:])
            width = PASS // calls
            for u in range(calls):
                cols = slice(u * width, (u + 1) * width)
                nc.vector.quantize_mx(
                    out=w1_codes[b, a][:, cols].bitcast(FP8X4),
                    scales=w1_sc[b, a][:, cols],
                    in_=rounded[:, PACK * u * width : PACK * (u + 1) * width],
                )

        def look(i):
            b, t = divmod(i, PACK)
            cols = slice(t * P, (t + 1) * P)
            h_sb = ring.tile([P, S], F32, name="h_sb")
            tops = ring.tile([P, HALVES], F32, name="tops")
            neg_top = ring.tile([P, 1], F32, name="neg_top")
            banks = [psum.tile([P, BANK], F32, name="bank%d" % (HALVES * (i % 2) + c)) for c in range(HALVES)]
            for a in range(K_PASSES):
                for c in range(HALVES):
                    js = slice(c * BANK, (c + 1) * BANK)
                    nc.tensor.matmul_mx(
                        out=banks[c][:],
                        lhsT=w1_codes[b, a][:, cols].bitcast(FP8X4),
                        lhsT_scale=w1_sc[b, a][:, cols],
                        rhs=v_words[a][:, js].bitcast(FP8X4),
                        rhs_scale=v_sc[SCALE_ROWS * a : P, js],
                        start=(a == 0),
                        stop=(a == K_PASSES - 1),
                    )
            for c in range(HALVES):
                nc.vector.tensor_scalar(
                    out=h_sb[:, c * BANK : (c + 1) * BANK],
                    in0=banks[c][:],
                    scalar1=1.0,
                    scalar2=tops[:, c - 1 : c] if c else None,
                    op0=ALU.mult,
                    op1=ALU.max,
                    accum_out=tops[:, c : c + 1],
                )
            nc.scalar.activation(out=neg_top[:], in_=tops[:, HALVES - 1 : HALVES], func=ACT.Copy, scale=-1.0)
            looked[i] = ring.tile([P, M], F32, name="looked", bufs=LOOK_BUFS)
            nc.scalar.activation(out=looked[i][:], in_=h_sb[:].indirect(pos1_sb[:]), func=ACT.Exp, bias=neg_top[:])
            page[i] = ring.tile([P, S], F32, name="page", bufs=PAGE_BUFS)
            nc.scalar.activation(out=page[i][:], in_=h_sb[:], func=ACT.Copy, scale=skip_sb[:, b, t : t + 1])

        def make_factor(i):
            factor[i] = ring.tile([P, M], F32, name="factor")
            nc.gpsimd.tensor_tensor(out=factor[i][:], in0=tint_sb[i], in1=wgs_sb[i % PACK][:], op=ALU.mult)

        def rewrite(i):
            nc.vector.tensor_tensor(out=page[i][:].indirect(pos2_sb[:]), in0=looked[i][:], in1=factor[i][:], op=ALU.mult)

        def round_page(i, j0=0, j1=S, on_vector=False):
            b, t = divmod(i, PACK)
            row_gain = gain_sb[:, b, t : t + 1]
            if on_vector:
                nc.vector.tensor_scalar(
                    out=b_rows[b][:, t, j0:j1], in0=page[i][:, j0:j1], scalar1=row_gain, scalar2=None, op0=ALU.mult
                )
            else:
                nc.scalar.activation(out=b_rows[b][:, t, j0:j1], in_=page[i][:, j0:j1], func=ACT.Copy, scale=row_gain)

        def weave(b, j0, on_vector=False):
            if j0 == 0:
                b_woven[b] = held.tile([P, S, PACK], BF16, name="b_woven", align_bytes=64)
            src = b_rows[b][:, :, j0 : j0 + QUARTER].rearrange("p t (c e) -> p c t e", e=4)
            dst = b_woven[b][:, j0 : j0 + QUARTER, :].rearrange("p (c e) t -> p c t e", e=4)
            if on_vector:
                nc.vector.tensor_copy(out=dst, in_=src)
            else:
                nc.scalar.copy(out=dst, in_=src)

        def quantise_page(b, j0, j1):
            nc.vector.quantize_mx(
                out=b_codes[b][:, j0:j1].bitcast(FP8X4),
                scales=b_sc[b][:, j0:j1],
                in_=b_woven[b][:, j0:j1, :].rearrange("p j t -> p (j t)"),
            )

        def second_product(b, u):
            j0, j1 = PIECES[u]
            for n in range(N_TILES):
                if b == 0:
                    acc[u, n] = psum.tile([P, j1 - j0], F32, name="bank%d" % (N_TILES * (1 - u % 2) + n))
                nc.tensor.matmul_mx(
                    out=acc[u, n][:],
                    lhsT=w4_sb[:, b, 2 * P * n : 2 * P * (n + 1)].bitcast(FP4X4),
                    lhsT_scale=w4_sc[:, b, P * n : P * (n + 1)],
                    rhs=b_codes[b][:, j0:j1].bitcast(FP8X4),
                    rhs_scale=b_sc[b][:, j0:j1],
                    start=(b == 0),
                    stop=(b == R_PASSES - 1),
                )

        def store(u, n0, n1, on_vector=False):
            j0, j1 = PIECES[u]
            result = held.tile([P, n1 - n0, j1 - j0], F32, name="result%d_%d" % (u, n0))
            for n in range(n0, n1):
                if on_vector:
                    nc.vector.tensor_copy(out=result[:, n - n0, :], in_=acc[u, n][:])
                else:
                    nc.scalar.copy(out=result[:, n - n0, :], in_=acc[u, n][:])
            nc.sync.dma_start(out=out[n0 * P : n1 * P, j0:j1].rearrange("(n p) j -> p n j", p=P), in_=result[:])

        nc.gpsimd.memset(tab_sc[:].bitcast(U32), 0)

        nc.sync.dma_start(offs_sb[:], offs)
        deal_wgs()
        load_tab(0)
        nc.sync.dma_start(pos2_sb[:], pos2)
        nc.sync.dma_start(pos1_sb[:], pos1)
        for quad in range(QUADRANTS):
            nc.sync.dma_start(
                out=tab_sc[QUADRANT * quad : QUADRANT * quad + SCALE_ROWS * K_PASSES, :].bitcast(I32),
                in_=tab_scales[:, SCALE_ROWS * quad : SCALE_ROWS * (quad + 1), :].bitcast(I32),
            )
        load_w1(0, 0)
        for a in range(1, K_PASSES):
            load_tab(a)
            load_w1(0, a)
        nc.sync.dma_start(out=skip_sb[:], in_=skip.rearrange("(b p t) -> p b t", p=P, t=PACK))
        load_w1(1, 0)
        load_tint(0, 0, 1)
        load_tint(0, 1, PACK - 1)
        for a in range(1, K_PASSES):
            load_w1(1, a)
        load_tint(0, PACK - 1, PACK)
        nc.sync.dma_start(out=gain_sb[:], in_=gain.rearrange("(b p t) -> p b t", p=P, t=PACK))
        load_tint(1, 0, PACK)

        gather_words(0)
        nc.vector.tensor_copy(out=v_sc[:], in_=tab_sc[:].indirect(offs_sb[:]))
        gather_words(1)
        quantise_w1(0, 0, 1)
        quantise_w1(0, 1, 1)
        gather_words(2)
        quantise_w1(0, 2, PACK)
        quantise_w1(1, 0, 1)

        nc.gpsimd.memset(w4_sc[:].rearrange("p b n -> p (b n)").bitcast(U32), 0)
        for b in range(R_PASSES):
            nc.sync.dma_start(out=w4_sb[:, b, :].bitcast(I32), in_=w4_words[b].bitcast(I32))
        for quad in range(QUADRANTS):
            nc.sync.dma_start(
                out=w4_sc[QUADRANT * quad : QUADRANT * quad + SCALE_ROWS, :, :].bitcast(I32),
                in_=w4_scales[:, SCALE_ROWS * quad : SCALE_ROWS * (quad + 1), :].rearrange("b r n -> r b n").bitcast(I32),
            )

        look(0)
        look(1)
        for i in range(2):
            make_factor(i)
            quantise_w1(1, i + 1, PACK if i + 2 == K_PASSES else 1)
            look(i + 2)
            rewrite(i)
        make_factor(2)
        rewrite(2)
        for i in range(3):
            round_page(i)
        look(4)
        make_factor(3)
        rewrite(3)
        look(5)
        round_page(3)

        for c in range(HALVES):
            make_factor(PACK + c)
            rewrite(PACK + c)
            weave(0, c * BANK)
            weave(0, c * BANK + QUARTER)
            quantise_page(0, c * BANK, (c + 1) * BANK)
            look(PACK + c + 2)
        round_page(4)
        second_product(0, 0)
        second_product(0, 1)
        round_page(5)
        last = ROW_TILES - 1
        make_factor(last - 1)
        rewrite(last - 1)
        round_page(last - 1)
        make_factor(last)
        rewrite(last)

        round_page(last, 0, QUARTER, on_vector=True)
        weave(1, 0, on_vector=True)
        quantise_page(1, *PIECES[0])
        second_product(1, 0)
        round_page(last, QUARTER, 2 * QUARTER)
        weave(1, QUARTER)
        round_page(last, 2 * QUARTER, 3 * QUARTER, on_vector=True)
        weave(1, 2 * QUARTER, on_vector=True)
        quantise_page(1, *PIECES[1])
        second_product(1, 1)
        store(0, 0, N_TILES // 2)
        round_page(last, 3 * QUARTER, S)
        store(0, N_TILES // 2, N_TILES)
        weave(1, 3 * QUARTER, on_vector=True)
        quantise_page(1, *PIECES[2])
        second_product(0, 2)
        second_product(1, 2)
        for n in range(N_TILES):
            store(1, n, n + 1, on_vector=(n >= N_TILES // 2))
        store(2, 0, N_TILES // 2)
        store(2, N_TILES // 2, N_TILES, on_vector=True)
